import numpy as np
import ml_dtypes


def mxq(x, axis, fmt="e4m3"):
    dtype, down = {"e4m3": (ml_dtypes.float8_e4m3fn, 7), "e5m2": (ml_dtypes.float8_e5m2, 14)}[fmt]
    v = np.moveaxis(np.asarray(x, np.float32).astype(ml_dtypes.bfloat16).astype(np.float64), axis, -1)
    blocks = v.reshape(v.shape[:-1] + (-1, 32))
    amax = np.abs(blocks).max(-1, keepdims=True)
    byte = np.maximum(np.where(amax > 0, np.frexp(amax)[1] - 1 + 127, 0) - down, 1)
    scale = np.exp2(byte - 127.0)
    codes = (blocks / scale).astype(np.float32).astype(dtype).astype(np.float64)
    return np.moveaxis((codes * scale).reshape(v.shape), -1, axis)


WIDE = False


def mx_kscale(k):
    if not WIDE:
        return np.ones(k)
    levels = np.array([10, -10, 5, -5, 0])
    if k % 512:
        return np.exp2(np.random.permutation(np.resize(levels, k // 32))).repeat(32)
    a = np.empty((k // 512, 16))
    for p in range(k // 512):
        a[p, :8] = np.random.permutation(np.resize(levels, 8))
        for g in range(8):
            far = levels[np.abs(levels - a[p, g]) >= 10]
            a[p, g + 8] = far[np.random.randint(len(far))]
    return np.exp2(a.ravel()).repeat(32)


def f64(x):
    return np.asarray(x).astype(np.float64)


def striped(idx):
    return np.tile(idx.reshape(-1, 16).T, (8, 1)).astype(np.uint16)


def unstriped(offs):
    return offs[:16].T.reshape(-1).astype(np.int64)


def pack_weight(w):
    k, n = w.shape
    w = f64(np.asarray(w, np.float32).astype(ml_dtypes.bfloat16)).reshape(k // 32, 32, n)
    amax = np.abs(w).max(1)
    byte = np.clip(np.where(amax > 0, np.frexp(amax)[1] - 1 + 127 - 7, 1), 1, 254)
    scaled = (w * np.exp2(127.0 - byte)[:, None, :]).reshape(k, n).astype(np.float32)
    words = np.ascontiguousarray(scaled.reshape(k // 512, 128, 4, n).transpose(0, 1, 3, 2)).astype(ml_dtypes.float8_e4m3fn).view(np.uint8)
    return words, np.ascontiguousarray(byte.astype(np.uint8).reshape(k // 512, 16, n))


def unpack_weight(words, scales):
    g, p, n, _ = words.shape
    vals = np.ascontiguousarray(words).view(ml_dtypes.float8_e4m3fn).astype(np.float64) * np.repeat(np.exp2(scales.astype(np.float64) - 127.0), 8, axis=1)[..., None]
    return vals.transpose(0, 1, 3, 2).reshape(g * 512, n)


K, T, S, V, D, R, W = 512, 4096, 1024, 512, 4, 256, 256


def setup_inputs():
    n = np.random.standard_normal
    s = mx_kscale(K)[:, None]
    packed_xT = pack_weight(n((K, T)) * s)
    return {
        "x_words": packed_xT[0],
        "x_scales": packed_xT[1],
        "hT": (n((K, V)) / np.sqrt(K) / s).astype(np.float32),
        "alpha": (n((V, R))).astype(np.float32),
        "beta": (n((V, R))).astype(np.float32),
        "prior": (n((V, W))).astype(np.float32),
        "offs": striped(np.random.permutation(T)[:S]),
        "st": striped(np.random.permutation(np.concatenate([np.arange(R), np.random.randint(0, R, S - R)]))),
        "en": striped(np.random.permutation(np.concatenate([np.arange(R), np.random.randint(0, R, S - R)]))),
        "one": striped(np.random.permutation(W)),
        "zero": striped(np.random.permutation(W)),
    }


def reference(x_words, x_scales, hT, alpha, beta, prior, offs, st, en, one, zero):
    hTq = mxq(f64(hT), 0, "e4m3")
    xq = unpack_weight(x_words, x_scales)[:, unstriped(offs)]
    y = hTq.T @ xq
    mt = y + f64(alpha)[:, unstriped(st)] + f64(beta)[:, unstriped(en)]
    mg = mt.reshape(len(mt), -1, D).max(axis=2)
    return 0.7 * (mg[:, unstriped(one)] - mg[:, unstriped(zero)] - f64(prior))

@@ -1,0 +1,189 @@
+from contextlib import ExitStack
+
+import concourse.mybir as mybir
+
+K, T, S, V, D, R, W = 512, 4096, 1024, 512, 4, 256, 256
+FLOPS = 2 * K * V * S
+
+F32 = mybir.dt.float32
+BF16 = mybir.dt.bfloat16
+I32 = mybir.dt.int32
+U32 = mybir.dt.uint32
+U16 = mybir.dt.uint16
+U8 = mybir.dt.uint8
+FP8X4 = mybir.dt.float8_e4m3fn_x4
+ALU = mybir.AluOpType
+COPY = mybir.ActivationFunctionType.Copy
+AXIS_X = mybir.AxisListType.X
+
+P = 128
+PACK = 4
+BLOCKS = V // P
+HALF = 512
+HALVES = S // HALF
+GROUPS = HALF // D
+STRIPE = 16
+GAIN = 0.7
+STATE_CUTS = (0, 192, 384, 512)
+BIT_CUTS = (0, 128, 256)
+
+
+def pieces(cuts):
+    return list(zip(cuts[:-1], cuts[1:]))
+
+
+def looked_up(window, offsets, first, last):
+    return window[:].indirect(offsets[:, first // STRIPE : last // STRIPE])
+
+
+def tile_picked_ybcjr_max_p_kernel(tc, x_words, x_scales, hT, alpha, beta, prior, offs, st, en, one, zero, out):
+    nc = tc.nc
+    with ExitStack() as ctx:
+        keep = ctx.enter_context(tc.tile_pool(name="keep", bufs=1))
+        ring = ctx.enter_context(tc.tile_pool(name="ring", bufs=3))
+        psum = ctx.enter_context(tc.psum_pool(name="psum", bufs=1))
+
+        def load_list(name, source):
+            tile = keep.tile(list(source.shape), U16, name=name)
+            nc.sync.dma_start(tile[:], source)
+            return tile
+
+        def load_rows(name, source, b):
+            tile = keep.tile([P, source.shape[1]], F32, name=f"{name}{b}")
+            nc.sync.dma_start(tile[:], source[b * P : (b + 1) * P, :])
+            return tile
+
+        def load_h(c):
+            tile = keep.tile([P, PACK, V // 2], F32, name=f"h_raw{c}")
+            nc.sync.dma_start(tile[:], hT[:, c * (V // 2) : (c + 1) * (V // 2)].rearrange("(p j) t -> p j t", j=PACK))
+            return tile
+
+        scale_table = keep.tile([P, T], U8, name="scale_table")
+        nc.vector.memset(scale_table[:].bitcast(I32), 0)
+
+        alphas, betas, priors, h_raw = {}, {}, {}, {}
+        st_list = load_list("st_list", st)
+        alphas[0] = load_rows("alpha", alpha, 0)
+        alphas[1] = load_rows("alpha", alpha, 1)
+        en_list = load_list("en_list", en)
+        betas[0] = load_rows("beta", beta, 0)
+        offs_list = load_list("offs_list", offs)
+        betas[1] = load_rows("beta", beta, 1)
+        word_table = keep.tile([P, T], U32, name="word_table")
+        nc.sync.dma_start(word_table[:].bitcast(I32), x_words[0].rearrange("p c r -> p (c r)").bitcast(I32))
+        h_raw[0] = load_h(0)
+        for q in range(4):
+            nc.sync.dma_start(scale_table[32 * q : 32 * q + 4, :].bitcast(I32), x_scales[0, 4 * q : 4 * q + 4, :].bitcast(I32))
+        h_raw[1] = load_h(1)
+        alphas[2] = load_rows("alpha", alpha, 2)
+        betas[2] = load_rows("beta", beta, 2)
+        alphas[3] = load_rows("alpha", alpha, 3)
+        betas[3] = load_rows("beta", beta, 3)
+        for b in range(BLOCKS):
+            priors[b] = load_rows("prior", prior, b)
+        one_list = load_list("one_list", one)
+        zero_list = load_list("zero_list", zero)
+
+        forward, both = {}, {}
+
+        def gather_forward(b, h, on_vector):
+            tile = keep.tile([P, HALF], F32, name=f"forward{b}_{h}")
+            for first, last in pieces(STATE_CUTS):
+                source = looked_up(alphas[b], st_list, h * HALF + first, h * HALF + last)
+                if on_vector:
+                    nc.vector.tensor_copy(tile[:, first:last], source)
+                else:
+                    nc.scalar.activation(tile[:, first:last], source, COPY)
+            forward[b, h] = tile
+
+        def add_backward(b, h, on_vector):
+            tile = keep.tile([P, HALF], F32, name=f"both{b}_{h}")
+            if on_vector:
+                for first, last in pieces(STATE_CUTS):
+                    source = looked_up(betas[b], en_list, h * HALF + first, h * HALF + last)
+                    nc.vector.tensor_tensor(tile[:, first:last], source, forward[b, h][:, first:last], ALU.add)
+            else:
+                backward = keep.tile([P, HALF], F32, name=f"backward{b}_{h}")
+                for first, last in pieces(STATE_CUTS):
+                    source = looked_up(betas[b], en_list, h * HALF + first, h * HALF + last)
+                    nc.scalar.activation(backward[:, first:last], source, COPY)
+                nc.gpsimd.tensor_tensor(tile[:], backward[:], forward[b, h][:], ALU.add)
+            both[b, h] = tile
+
+        gather_forward(0, 0, True)
+        gather_forward(0, 1, True)
+        add_backward(0, 0, True)
+        add_backward(0, 1, True)
+        gather_forward(1, 0, False)
+        gather_forward(1, 1, False)
+
+        x_codes, x_bytes = {}, {}
+        for h in range(HALVES):
+            x_codes[h] = keep.tile([P, HALF], U32, name=f"x_codes{h}", align_bytes=64)
+            nc.vector.tensor_copy(x_codes[h][:], looked_up(word_table, offs_list, h * HALF, (h + 1) * HALF))
+        for h in range(HALVES):
+            x_bytes[h] = keep.tile([P, HALF], U8, name=f"x_bytes{h}", align_bytes=64)
+            nc.vector.tensor_copy(x_bytes[h][:], looked_up(scale_table, offs_list, h * HALF, (h + 1) * HALF))
+
+        h_codes, h_bytes = {}, {}
+        for c in range(2):
+            rounded = keep.tile([P, V // 2, PACK], BF16, name=f"h_rounded{c}", align_bytes=64)
+            nc.gpsimd.tensor_scalar(rounded[:], h_raw[c][:].rearrange("p j t -> p t j"), 1.0, 0.0, ALU.mult, ALU.add)
+            h_codes[c] = keep.tile([P, V // 2], U32, name=f"h_codes{c}", align_bytes=64)
+            h_bytes[c] = keep.tile([P, V // 2], U8, name=f"h_bytes{c}", align_bytes=64)
+            nc.vector.quantize_mx(out=h_codes[c][:].bitcast(FP8X4), scales=h_bytes[c][:], in_=rounded[:].rearrange("p t j -> p (t j)"))
+
+        add_backward(1, 0, False)
+        add_backward(1, 1, False)
+        for b in range(2, BLOCKS):
+            for h in range(HALVES):
+                gather_forward(b, h, False)
+                add_backward(b, h, False)
+
+        best = {}
+        for b in range(BLOCKS):
+            best[b] = keep.tile([P, W], F32, name=f"best{b}")
+            c, cols = b // 2, slice((b % 2) * P, (b % 2 + 1) * P)
+            metrics = []
+            for h in range(HALVES):
+                y = psum.tile([P, HALF], F32, name=f"y{b}_{h}")
+                nc.tensor.matmul_mx(
+                    out=y[:],
+                    lhsT=h_codes[c][:, cols].bitcast(FP8X4),
+                    lhsT_scale=h_bytes[c][:, cols],
+                    rhs=x_codes[h][:].bitcast(FP8X4),
+                    rhs_scale=x_bytes[h][:],
+                    start=True,
+                    stop=True,
+                )
+                metric = ring.tile([P, HALF], F32, name="metric")
+                nc.vector.tensor_tensor(metric[:], y[:], both[b, h][:], ALU.add)
+                metrics.append(metric)
+            for h in range(HALVES):
+                nc.vector.tensor_reduce(
+                    best[b][:, h * GROUPS : (h + 1) * GROUPS],
+                    metrics[h][:].rearrange("p (g d) -> p g d", d=D),
+                    AXIS_X,
+                    ALU.max,
+                )
+
+        for b in range(BLOCKS):
+            ones = keep.tile([P, W], F32, name=f"ones{b}")
+            result = keep.tile([P, W], F32, name=f"result{b}")
+            for first, last in pieces(BIT_CUTS):
+                nc.scalar.activation(ones[:, first:last], looked_up(best[b], one_list, first, last), COPY, scale=GAIN)
+            if b < BLOCKS - 1:
+                scaled = keep.tile([P, W], F32, name=f"scaled{b}")
+                nc.gpsimd.tensor_scalar(scaled[:], priors[b][:], GAIN, 0.0, ALU.mult, ALU.add)
+                zeros = keep.tile([P, W], F32, name=f"zeros{b}")
+                for first, last in pieces(BIT_CUTS):
+                    nc.scalar.activation(zeros[:, first:last], looked_up(best[b], zero_list, first, last), COPY, scale=GAIN)
+                part = keep.tile([P, W], F32, name=f"part{b}")
+                nc.gpsimd.tensor_tensor(part[:], ones[:], scaled[:], ALU.subtract)
+                nc.gpsimd.tensor_tensor(result[:], part[:], zeros[:], ALU.subtract)
+            else:
+                part = keep.tile([P, W], F32, name=f"part{b}")
+                for first, last in pieces(BIT_CUTS):
+                    nc.vector.tensor_tensor(part[:, first:last], looked_up(best[b], zero_list, first, last), priors[b][:, first:last], ALU.add)
+                nc.vector.scalar_tensor_tensor(result[:], part[:], -GAIN, ones[:], ALU.mult, ALU.add)
+            nc.sync.dma_start(out[b * P : (b + 1) * P, :], result[:])

@@ -19,21 +19,18 @@ AXIS_X = mybir.AxisListType.X
 P = 128
 PACK = 4
 BLOCKS = V // P
+LAST = BLOCKS - 1
 HALF = 512
 HALVES = S // HALF
 GROUPS = HALF // D
 STRIPE = 16
 GAIN = 0.7
-STATE_CUTS = (0, 192, 384, 512)
-BIT_CUTS = (0, 128, 256)
+STATE_WINDOW = HALF + STRIPE
+BIT_WINDOW = W + STRIPE
 
 
-def pieces(cuts):
-    return list(zip(cuts[:-1], cuts[1:]))
-
-
-def looked_up(window, offsets, first, last):
-    return window[:].indirect(offsets[:, first // STRIPE : last // STRIPE])
+def looked_up(window, offsets, first, count):
+    return window[:].indirect(offsets[:, first // STRIPE : (first + count) // STRIPE])
 
 
 def tile_picked_ybcjr_max_p_kernel(tc, x_words, x_scales, hT, alpha, beta, prior, offs, st, en, one, zero, out):
@@ -48,9 +45,10 @@ def tile_picked_ybcjr_max_p_kernel(tc, x_words, x_scales, hT, alpha, beta, prior
             nc.sync.dma_start(tile[:], source)
             return tile
 
-        def load_rows(name, source, b):
-            tile = keep.tile([P, source.shape[1]], F32, name=f"{name}{b}")
-            nc.sync.dma_start(tile[:], source[b * P : (b + 1) * P, :])
+        def load_states(name, source, b):
+            tile = keep.tile([P, STATE_WINDOW], F32, name=f"{name}{b}")
+            nc.gpsimd.memset(tile[:, R:], 0.0)
+            nc.sync.dma_start(tile[:, :R], source[b * P : (b + 1) * P, :])
             return tile
 
         def load_h(c):
@@ -61,88 +59,75 @@ def tile_picked_ybcjr_max_p_kernel(tc, x_words, x_scales, hT, alpha, beta, prior
         scale_table = keep.tile([P, T], U8, name="scale_table")
         nc.vector.memset(scale_table[:].bitcast(I32), 0)
 
-        alphas, betas, priors, h_raw = {}, {}, {}, {}
+        alphas, betas, h_raw = {}, {}, {}
         st_list = load_list("st_list", st)
-        alphas[0] = load_rows("alpha", alpha, 0)
-        alphas[1] = load_rows("alpha", alpha, 1)
+        alphas[0] = load_states("alpha", alpha, 0)
+        alphas[1] = load_states("alpha", alpha, 1)
         en_list = load_list("en_list", en)
-        betas[0] = load_rows("beta", beta, 0)
+        betas[0] = load_states("beta", beta, 0)
         offs_list = load_list("offs_list", offs)
-        betas[1] = load_rows("beta", beta, 1)
+        alphas[2] = load_states("alpha", alpha, 2)
         word_table = keep.tile([P, T], U32, name="word_table")
         nc.sync.dma_start(word_table[:].bitcast(I32), x_words[0].rearrange("p c r -> p (c r)").bitcast(I32))
-        h_raw[0] = load_h(0)
+        alphas[3] = load_states("alpha", alpha, 3)
         for q in range(4):
             nc.sync.dma_start(scale_table[32 * q : 32 * q + 4, :].bitcast(I32), x_scales[0, 4 * q : 4 * q + 4, :].bitcast(I32))
+        h_raw[0] = load_h(0)
+        betas[1] = load_states("beta", beta, 1)
         h_raw[1] = load_h(1)
-        alphas[2] = load_rows("alpha", alpha, 2)
-        betas[2] = load_rows("beta", beta, 2)
-        alphas[3] = load_rows("alpha", alpha, 3)
-        betas[3] = load_rows("beta", beta, 3)
-        for b in range(BLOCKS):
-            priors[b] = load_rows("prior", prior, b)
+        betas[2] = load_states("beta", beta, 2)
+        betas[3] = load_states("beta", beta, 3)
+        priors = keep.tile([P, BLOCKS, W], F32, name="priors")
+        nc.sync.dma_start(priors[:], prior.rearrange("(b p) g -> p b g", p=P))
         one_list = load_list("one_list", one)
         zero_list = load_list("zero_list", zero)
 
+        best = {}
+        for b in range(BLOCKS):
+            best[b] = keep.tile([P, BIT_WINDOW], F32, name=f"best{b}")
+            nc.gpsimd.memset(best[b][:, W:], 0.0)
+
         forward, both = {}, {}
+        for b in range(BLOCKS):
+            for h in range(HALVES):
+                forward[b, h] = keep.tile([P, HALF], F32, name=f"forward{b}_{h}")
+                both[b, h] = keep.tile([P, HALF], F32, name=f"both{b}_{h}")
 
-        def gather_forward(b, h, on_vector):
-            tile = keep.tile([P, HALF], F32, name=f"forward{b}_{h}")
-            for first, last in pieces(STATE_CUTS):
-                source = looked_up(alphas[b], st_list, h * HALF + first, h * HALF + last)
-                if on_vector:
-                    nc.vector.tensor_copy(tile[:, first:last], source)
-                else:
-                    nc.scalar.activation(tile[:, first:last], source, COPY)
-            forward[b, h] = tile
-
-        def add_backward(b, h, on_vector):
-            tile = keep.tile([P, HALF], F32, name=f"both{b}_{h}")
-            if on_vector:
-                for first, last in pieces(STATE_CUTS):
-                    source = looked_up(betas[b], en_list, h * HALF + first, h * HALF + last)
-                    nc.vector.tensor_tensor(tile[:, first:last], source, forward[b, h][:, first:last], ALU.add)
-            else:
-                backward = keep.tile([P, HALF], F32, name=f"backward{b}_{h}")
-                for first, last in pieces(STATE_CUTS):
-                    source = looked_up(betas[b], en_list, h * HALF + first, h * HALF + last)
-                    nc.scalar.activation(backward[:, first:last], source, COPY)
-                nc.gpsimd.tensor_tensor(tile[:], backward[:], forward[b, h][:], ALU.add)
-            both[b, h] = tile
-
-        gather_forward(0, 0, True)
-        gather_forward(0, 1, True)
-        add_backward(0, 0, True)
-        add_backward(0, 1, True)
-        gather_forward(1, 0, False)
-        gather_forward(1, 1, False)
+        for h in range(HALVES):
+            nc.vector.tensor_copy(forward[0, h][:], looked_up(alphas[0], st_list, h * HALF, HALF))
+        for h in range(HALVES):
+            nc.vector.tensor_tensor(both[0, h][:], looked_up(betas[0], en_list, h * HALF, HALF), forward[0, h][:], ALU.add)
+        for b in range(1, BLOCKS):
+            for h in range(HALVES):
+                nc.scalar.activation(forward[b, h][:], looked_up(alphas[b], st_list, h * HALF, HALF), COPY)
 
         x_codes, x_bytes = {}, {}
         for h in range(HALVES):
             x_codes[h] = keep.tile([P, HALF], U32, name=f"x_codes{h}", align_bytes=64)
-            nc.vector.tensor_copy(x_codes[h][:], looked_up(word_table, offs_list, h * HALF, (h + 1) * HALF))
+            nc.vector.tensor_copy(x_codes[h][:], looked_up(word_table, offs_list, h * HALF, HALF))
         for h in range(HALVES):
             x_bytes[h] = keep.tile([P, HALF], U8, name=f"x_bytes{h}", align_bytes=64)
-            nc.vector.tensor_copy(x_bytes[h][:], looked_up(scale_table, offs_list, h * HALF, (h + 1) * HALF))
+            nc.vector.tensor_copy(x_bytes[h][:], looked_up(scale_table, offs_list, h * HALF, HALF))
 
-        h_codes, h_bytes = {}, {}
+        h_codes, h_bytes, rounded = {}, {}, {}
         for c in range(2):
-            rounded = keep.tile([P, V // 2, PACK], BF16, name=f"h_rounded{c}", align_bytes=64)
-            nc.gpsimd.tensor_scalar(rounded[:], h_raw[c][:].rearrange("p j t -> p t j"), 1.0, 0.0, ALU.mult, ALU.add)
+            rounded[c] = keep.tile([P, V // 2, PACK], BF16, name=f"h_rounded{c}", align_bytes=64)
+            nc.vector.tensor_copy(
+                rounded[c][:].rearrange("p (c i) j -> p c j i", i=4),
+                h_raw[c][:].rearrange("p j (c i) -> p c j i", i=4),
+            )
+        for c in range(2):
             h_codes[c] = keep.tile([P, V // 2], U32, name=f"h_codes{c}", align_bytes=64)
             h_bytes[c] = keep.tile([P, V // 2], U8, name=f"h_bytes{c}", align_bytes=64)
-            nc.vector.quantize_mx(out=h_codes[c][:].bitcast(FP8X4), scales=h_bytes[c][:], in_=rounded[:].rearrange("p t j -> p (t j)"))
+            nc.vector.quantize_mx(out=h_codes[c][:].bitcast(FP8X4), scales=h_bytes[c][:], in_=rounded[c][:].rearrange("p t j -> p (t j)"))
 
-        add_backward(1, 0, False)
-        add_backward(1, 1, False)
-        for b in range(2, BLOCKS):
+        for b in range(1, BLOCKS):
             for h in range(HALVES):
-                gather_forward(b, h, False)
-                add_backward(b, h, False)
+                backward = keep.tile([P, HALF], F32, name=f"backward{b}_{h}")
+                nc.scalar.activation(backward[:], looked_up(betas[b], en_list, h * HALF, HALF), COPY)
+                nc.gpsimd.tensor_tensor(both[b, h][:], backward[:], forward[b, h][:], ALU.add)
 
-        best = {}
         for b in range(BLOCKS):
-            best[b] = keep.tile([P, W], F32, name=f"best{b}")
             c, cols = b // 2, slice((b % 2) * P, (b % 2 + 1) * P)
             metrics = []
             for h in range(HALVES):
@@ -167,23 +152,19 @@ def tile_picked_ybcjr_max_p_kernel(tc, x_words, x_scales, hT, alpha, beta, prior
                     ALU.max,
                 )
 
+        scaled = keep.tile([P, LAST, W], F32, name="scaled")
+        nc.scalar.activation(scaled[:], priors[:, :LAST, :], COPY, scale=GAIN)
         for b in range(BLOCKS):
             ones = keep.tile([P, W], F32, name=f"ones{b}")
+            part = keep.tile([P, W], F32, name=f"part{b}")
             result = keep.tile([P, W], F32, name=f"result{b}")
-            for first, last in pieces(BIT_CUTS):
-                nc.scalar.activation(ones[:, first:last], looked_up(best[b], one_list, first, last), COPY, scale=GAIN)
-            if b < BLOCKS - 1:
-                scaled = keep.tile([P, W], F32, name=f"scaled{b}")
-                nc.gpsimd.tensor_scalar(scaled[:], priors[b][:], GAIN, 0.0, ALU.mult, ALU.add)
+            nc.scalar.activation(ones[:], looked_up(best[b], one_list, 0, W), COPY, scale=GAIN)
+            if b < LAST:
                 zeros = keep.tile([P, W], F32, name=f"zeros{b}")
-                for first, last in pieces(BIT_CUTS):
-                    nc.scalar.activation(zeros[:, first:last], looked_up(best[b], zero_list, first, last), COPY, scale=GAIN)
-                part = keep.tile([P, W], F32, name=f"part{b}")
-                nc.gpsimd.tensor_tensor(part[:], ones[:], scaled[:], ALU.subtract)
+                nc.scalar.activation(zeros[:], looked_up(best[b], zero_list, 0, W), COPY, scale=GAIN)
+                nc.gpsimd.tensor_tensor(part[:], ones[:], scaled[:, b, :], ALU.subtract)
                 nc.gpsimd.tensor_tensor(result[:], part[:], zeros[:], ALU.subtract)
             else:
-                part = keep.tile([P, W], F32, name=f"part{b}")
-                for first, last in pieces(BIT_CUTS):
-                    nc.vector.tensor_tensor(part[:, first:last], looked_up(best[b], zero_list, first, last), priors[b][:, first:last], ALU.add)
+                nc.vector.tensor_tensor(part[:], looked_up(best[b], zero_list, 0, W), priors[:, b, :], ALU.add)
                 nc.vector.scalar_tensor_tensor(result[:], part[:], -GAIN, ones[:], ALU.mult, ALU.add)
             nc.sync.dma_start(out[b * P : (b + 1) * P, :], result[:])

@@ -14,15 +14,12 @@ U8 = mybir.dt.uint8
 FP8X4 = mybir.dt.float8_e4m3fn_x4
 ALU = mybir.AluOpType
 COPY = mybir.ActivationFunctionType.Copy
-AXIS_X = mybir.AxisListType.X
 
 P = 128
 PACK = 4
 BLOCKS = V // P
-LAST = BLOCKS - 1
 HALF = 512
 HALVES = S // HALF
-GROUPS = HALF // D
 STRIPE = 16
 GAIN = 0.7
 STATE_WINDOW = HALF + STRIPE
@@ -37,7 +34,6 @@ def tile_picked_ybcjr_max_p_kernel(tc, x_words, x_scales, hT, alpha, beta, prior
     nc = tc.nc
     with ExitStack() as ctx:
         keep = ctx.enter_context(tc.tile_pool(name="keep", bufs=1))
-        ring = ctx.enter_context(tc.tile_pool(name="ring", bufs=3))
         psum = ctx.enter_context(tc.psum_pool(name="psum", bufs=1))
 
         def load_list(name, source):
@@ -47,7 +43,7 @@ def tile_picked_ybcjr_max_p_kernel(tc, x_words, x_scales, hT, alpha, beta, prior
 
         def load_states(name, source, b):
             tile = keep.tile([P, STATE_WINDOW], F32, name=f"{name}{b}")
-            nc.gpsimd.memset(tile[:, R:], 0.0)
+            nc.vector.memset(tile[:, R:], 0.0)
             nc.sync.dma_start(tile[:, :R], source[b * P : (b + 1) * P, :])
             return tile
 
@@ -56,27 +52,29 @@ def tile_picked_ybcjr_max_p_kernel(tc, x_words, x_scales, hT, alpha, beta, prior
             nc.sync.dma_start(tile[:], hT[:, c * (V // 2) : (c + 1) * (V // 2)].rearrange("(p j) t -> p j t", j=PACK))
             return tile
 
-        scale_table = keep.tile([P, T], U8, name="scale_table")
-        nc.vector.memset(scale_table[:].bitcast(I32), 0)
+        warm = keep.tile([P, 8], F32, name="warm")
+        nc.gpsimd.memset(warm[:, 0:1], 0.0)
+        nc.scalar.activation(warm[:, 4:5], warm[:, 0:1], COPY)
 
         alphas, betas, h_raw = {}, {}, {}
         st_list = load_list("st_list", st)
         alphas[0] = load_states("alpha", alpha, 0)
-        alphas[1] = load_states("alpha", alpha, 1)
         en_list = load_list("en_list", en)
         betas[0] = load_states("beta", beta, 0)
+        alphas[1] = load_states("alpha", alpha, 1)
         offs_list = load_list("offs_list", offs)
-        alphas[2] = load_states("alpha", alpha, 2)
         word_table = keep.tile([P, T], U32, name="word_table")
         nc.sync.dma_start(word_table[:].bitcast(I32), x_words[0].rearrange("p c r -> p (c r)").bitcast(I32))
-        alphas[3] = load_states("alpha", alpha, 3)
+        alphas[2] = load_states("alpha", alpha, 2)
+        scale_table = keep.tile([P, T], U8, name="scale_table")
+        nc.vector.memset(scale_table[:].bitcast(I32), 0)
         for q in range(4):
             nc.sync.dma_start(scale_table[32 * q : 32 * q + 4, :].bitcast(I32), x_scales[0, 4 * q : 4 * q + 4, :].bitcast(I32))
         h_raw[0] = load_h(0)
-        betas[1] = load_states("beta", beta, 1)
+        alphas[3] = load_states("alpha", alpha, 3)
         h_raw[1] = load_h(1)
-        betas[2] = load_states("beta", beta, 2)
-        betas[3] = load_states("beta", beta, 3)
+        for b in range(1, BLOCKS):
+            betas[b] = load_states("beta", beta, b)
         priors = keep.tile([P, BLOCKS, W], F32, name="priors")
         nc.sync.dma_start(priors[:], prior.rearrange("(b p) g -> p b g", p=P))
         one_list = load_list("one_list", one)
@@ -85,51 +83,55 @@ def tile_picked_ybcjr_max_p_kernel(tc, x_words, x_scales, hT, alpha, beta, prior
         best = {}
         for b in range(BLOCKS):
             best[b] = keep.tile([P, BIT_WINDOW], F32, name=f"best{b}")
-            nc.gpsimd.memset(best[b][:, W:], 0.0)
+            nc.vector.memset(best[b][:, W:], 0.0)
 
-        forward, both = {}, {}
+        x_codes, x_bytes = {}, {}
+        forward, backward = {}, {}
         for b in range(BLOCKS):
             for h in range(HALVES):
                 forward[b, h] = keep.tile([P, HALF], F32, name=f"forward{b}_{h}")
-                both[b, h] = keep.tile([P, HALF], F32, name=f"both{b}_{h}")
-
+                if (b, h) == (0, 1):
+                    nc.vector.tensor_copy(forward[b, h][:], looked_up(alphas[b], st_list, h * HALF, HALF))
+                else:
+                    nc.scalar.activation(forward[b, h][:], looked_up(alphas[b], st_list, h * HALF, HALF), COPY)
         for h in range(HALVES):
-            nc.vector.tensor_copy(forward[0, h][:], looked_up(alphas[0], st_list, h * HALF, HALF))
-        for h in range(HALVES):
-            nc.vector.tensor_tensor(both[0, h][:], looked_up(betas[0], en_list, h * HALF, HALF), forward[0, h][:], ALU.add)
-        for b in range(1, BLOCKS):
-            for h in range(HALVES):
-                nc.scalar.activation(forward[b, h][:], looked_up(alphas[b], st_list, h * HALF, HALF), COPY)
+            backward[0, h] = keep.tile([P, HALF], F32, name=f"backward0_{h}")
+            nc.vector.tensor_tensor(backward[0, h][:], looked_up(betas[0], en_list, h * HALF, HALF), forward[0, h][:], ALU.add)
 
-        x_codes, x_bytes = {}, {}
         for h in range(HALVES):
             x_codes[h] = keep.tile([P, HALF], U32, name=f"x_codes{h}", align_bytes=64)
             nc.vector.tensor_copy(x_codes[h][:], looked_up(word_table, offs_list, h * HALF, HALF))
+
         for h in range(HALVES):
             x_bytes[h] = keep.tile([P, HALF], U8, name=f"x_bytes{h}", align_bytes=64)
             nc.vector.tensor_copy(x_bytes[h][:], looked_up(scale_table, offs_list, h * HALF, HALF))
 
-        h_codes, h_bytes, rounded = {}, {}, {}
+        h_codes, h_bytes = {}, {}
         for c in range(2):
-            rounded[c] = keep.tile([P, V // 2, PACK], BF16, name=f"h_rounded{c}", align_bytes=64)
-            nc.vector.tensor_copy(
-                rounded[c][:].rearrange("p (c i) j -> p c j i", i=4),
+            rounded = keep.tile([P, V // 2, PACK], BF16, name=f"h_rounded{c}", align_bytes=64)
+            (nc.scalar.copy if c in [0,1] else nc.vector.tensor_copy)(
+                rounded[:].rearrange("p (c i) j -> p c j i", i=4),
                 h_raw[c][:].rearrange("p j (c i) -> p c j i", i=4),
             )
-        for c in range(2):
             h_codes[c] = keep.tile([P, V // 2], U32, name=f"h_codes{c}", align_bytes=64)
             h_bytes[c] = keep.tile([P, V // 2], U8, name=f"h_bytes{c}", align_bytes=64)
-            nc.vector.quantize_mx(out=h_codes[c][:].bitcast(FP8X4), scales=h_bytes[c][:], in_=rounded[c][:].rearrange("p t j -> p (t j)"))
+            nc.vector.quantize_mx(out=h_codes[c][:].bitcast(FP8X4), scales=h_bytes[c][:], in_=rounded[:].rearrange("p t j -> p (t j)"))
 
         for b in range(1, BLOCKS):
             for h in range(HALVES):
-                backward = keep.tile([P, HALF], F32, name=f"backward{b}_{h}")
-                nc.scalar.activation(backward[:], looked_up(betas[b], en_list, h * HALF, HALF), COPY)
-                nc.gpsimd.tensor_tensor(both[b, h][:], backward[:], forward[b, h][:], ALU.add)
+                backward[b, h] = keep.tile([P, HALF], F32, name=f"backward{b}_{h}")
+                nc.scalar.activation(backward[b, h][:], looked_up(betas[b], en_list, h * HALF, HALF), COPY)
 
+        def largest_of_groups(b):
+            pairs = keep.tile([P, W, 2], F32, name=f"pairs{b}")
+            quads = metric[b][:].rearrange("p (g u e) -> p g u e", u=2, e=2)
+            nc.vector.tensor_tensor(pairs[:], quads[:, :, 0, :], quads[:, :, 1, :], ALU.max)
+            nc.vector.tensor_tensor(best[b][:, :W], pairs[:, :, 0], pairs[:, :, 1], ALU.max)
+
+        metric, started = {}, {}
         for b in range(BLOCKS):
             c, cols = b // 2, slice((b % 2) * P, (b % 2 + 1) * P)
-            metrics = []
+            metric[b] = keep.tile([P, S], F32, name=f"metric{b}")
             for h in range(HALVES):
                 y = psum.tile([P, HALF], F32, name=f"y{b}_{h}")
                 nc.tensor.matmul_mx(
@@ -141,29 +143,28 @@ def tile_picked_ybcjr_max_p_kernel(tc, x_words, x_scales, hT, alpha, beta, prior
                     start=True,
                     stop=True,
                 )
-                metric = ring.tile([P, HALF], F32, name="metric")
-                nc.vector.tensor_tensor(metric[:], y[:], both[b, h][:], ALU.add)
-                metrics.append(metric)
+                if b == 0:
+                    nc.vector.tensor_tensor(metric[b][:, h * HALF : (h + 1) * HALF], y[:], backward[b, h][:], ALU.add)
+                else:
+                    started[b, h] = keep.tile([P, HALF], F32, name=f"started{b}_{h}")
+                    nc.vector.tensor_tensor(started[b, h][:], y[:], forward[b, h][:], ALU.add)
+            if b == 0:
+                largest_of_groups(b)
+        for b in range(1, BLOCKS):
             for h in range(HALVES):
-                nc.vector.tensor_reduce(
-                    best[b][:, h * GROUPS : (h + 1) * GROUPS],
-                    metrics[h][:].rearrange("p (g d) -> p g d", d=D),
-                    AXIS_X,
-                    ALU.max,
-                )
+                nc.vector.tensor_tensor(metric[b][:, h * HALF : (h + 1) * HALF], started[b, h][:], backward[b, h][:], ALU.add)
+            largest_of_groups(b)
 
-        scaled = keep.tile([P, LAST, W], F32, name="scaled")
-        nc.scalar.activation(scaled[:], priors[:, :LAST, :], COPY, scale=GAIN)
         for b in range(BLOCKS):
             ones = keep.tile([P, W], F32, name=f"ones{b}")
             part = keep.tile([P, W], F32, name=f"part{b}")
             result = keep.tile([P, W], F32, name=f"result{b}")
             nc.scalar.activation(ones[:], looked_up(best[b], one_list, 0, W), COPY, scale=GAIN)
-            if b < LAST:
+            if b < 3:
                 zeros = keep.tile([P, W], F32, name=f"zeros{b}")
                 nc.scalar.activation(zeros[:], looked_up(best[b], zero_list, 0, W), COPY, scale=GAIN)
-                nc.gpsimd.tensor_tensor(part[:], ones[:], scaled[:, b, :], ALU.subtract)
-                nc.gpsimd.tensor_tensor(result[:], part[:], zeros[:], ALU.subtract)
+                nc.vector.scalar_tensor_tensor(part[:], priors[:, b, :], -GAIN, ones[:], ALU.mult, ALU.add)
+                nc.vector.tensor_tensor(result[:], part[:], zeros[:], ALU.subtract)
             else:
                 nc.vector.tensor_tensor(part[:], looked_up(best[b], zero_list, 0, W), priors[:, b, :], ALU.add)
                 nc.vector.scalar_tensor_tensor(result[:], part[:], -GAIN, ones[:], ALU.mult, ALU.add)

@@ -43,7 +43,7 @@ def tile_picked_ybcjr_max_p_kernel(tc, x_words, x_scales, hT, alpha, beta, prior
 
         def load_states(name, source, b):
             tile = keep.tile([P, STATE_WINDOW], F32, name=f"{name}{b}")
-            nc.vector.memset(tile[:, R:], 0.0)
+            (nc.vector if b == 0 else nc.gpsimd).memset(tile[:, R:], 0.0)
             nc.sync.dma_start(tile[:, :R], source[b * P : (b + 1) * P, :])
             return tile
 
@@ -62,6 +62,7 @@ def tile_picked_ybcjr_max_p_kernel(tc, x_words, x_scales, hT, alpha, beta, prior
         en_list = load_list("en_list", en)
         betas[0] = load_states("beta", beta, 0)
         alphas[1] = load_states("alpha", alpha, 1)
+        betas[1] = load_states("beta", beta, 1)
         offs_list = load_list("offs_list", offs)
         word_table = keep.tile([P, T], U32, name="word_table")
         nc.sync.dma_start(word_table[:].bitcast(I32), x_words[0].rearrange("p c r -> p (c r)").bitcast(I32))
@@ -73,7 +74,7 @@ def tile_picked_ybcjr_max_p_kernel(tc, x_words, x_scales, hT, alpha, beta, prior
         h_raw[0] = load_h(0)
         alphas[3] = load_states("alpha", alpha, 3)
         h_raw[1] = load_h(1)
-        for b in range(1, BLOCKS):
+        for b in range(2, BLOCKS):
             betas[b] = load_states("beta", beta, b)
         priors = keep.tile([P, BLOCKS, W], F32, name="priors")
         nc.sync.dma_start(priors[:], prior.rearrange("(b p) g -> p b g", p=P))
@@ -83,20 +84,35 @@ def tile_picked_ybcjr_max_p_kernel(tc, x_words, x_scales, hT, alpha, beta, prior
         best = {}
         for b in range(BLOCKS):
             best[b] = keep.tile([P, BIT_WINDOW], F32, name=f"best{b}")
-            nc.vector.memset(best[b][:, W:], 0.0)
+            nc.gpsimd.memset(best[b][:, W:], 0.0)
 
         x_codes, x_bytes = {}, {}
         forward, backward = {}, {}
-        for b in range(BLOCKS):
+        fused = [(0, 0), (0, 1), (1, 0)]
+
+        def gather_forward(b, h):
+            forward[b, h] = keep.tile([P, HALF], F32, name=f"forward{b}_{h}")
+            if (b, h) == (0, 1):
+                nc.vector.tensor_copy(forward[b, h][:], looked_up(alphas[b], st_list, h * HALF, HALF))
+            else:
+                nc.scalar.activation(forward[b, h][:], looked_up(alphas[b], st_list, h * HALF, HALF), COPY)
+
+        def gather_backward(b, h):
+            backward[b, h] = keep.tile([P, HALF], F32, name=f"backward{b}_{h}")
+            if (b, h) in fused:
+                nc.vector.tensor_tensor(backward[b, h][:], looked_up(betas[b], en_list, h * HALF, HALF), forward[b, h][:], ALU.add)
+            else:
+                nc.scalar.activation(backward[b, h][:], looked_up(betas[b], en_list, h * HALF, HALF), COPY)
+
+        for b in range(2):
             for h in range(HALVES):
-                forward[b, h] = keep.tile([P, HALF], F32, name=f"forward{b}_{h}")
-                if (b, h) == (0, 1):
-                    nc.vector.tensor_copy(forward[b, h][:], looked_up(alphas[b], st_list, h * HALF, HALF))
-                else:
-                    nc.scalar.activation(forward[b, h][:], looked_up(alphas[b], st_list, h * HALF, HALF), COPY)
-        for h in range(HALVES):
-            backward[0, h] = keep.tile([P, HALF], F32, name=f"backward0_{h}")
-            nc.vector.tensor_tensor(backward[0, h][:], looked_up(betas[0], en_list, h * HALF, HALF), forward[0, h][:], ALU.add)
+                gather_forward(b, h)
+        for b in range(2):
+            for h in range(HALVES):
+                gather_backward(b, h)
+        for b in range(2, BLOCKS):
+            for h in range(HALVES):
+                gather_forward(b, h)
 
         for h in range(HALVES):
             x_codes[h] = keep.tile([P, HALF], U32, name=f"x_codes{h}", align_bytes=64)
@@ -108,7 +124,7 @@ def tile_picked_ybcjr_max_p_kernel(tc, x_words, x_scales, hT, alpha, beta, prior
 
         h_codes, h_bytes = {}, {}
         for c in range(2):
-            rounded = keep.tile([P, V // 2, PACK], BF16, name=f"h_rounded{c}", align_bytes=64)
+            rounded = keep.tile([P, V // 2, PACK], BF16, name=f"h_rounded{c}", tag=f"h_rounded{c}", align_bytes=64)
             (nc.scalar.copy if c in [0,1] else nc.vector.tensor_copy)(
                 rounded[:].rearrange("p (c i) j -> p c j i", i=4),
                 h_raw[c][:].rearrange("p j (c i) -> p c j i", i=4),
@@ -117,21 +133,17 @@ def tile_picked_ybcjr_max_p_kernel(tc, x_words, x_scales, hT, alpha, beta, prior
             h_bytes[c] = keep.tile([P, V // 2], U8, name=f"h_bytes{c}", align_bytes=64)
             nc.vector.quantize_mx(out=h_codes[c][:].bitcast(FP8X4), scales=h_bytes[c][:], in_=rounded[:].rearrange("p t j -> p (t j)"))
 
-        for b in range(1, BLOCKS):
+        both = keep.tile([P, HALF], F32, name="both", tag="h_rounded0", align_bytes=64)
+        nc.vector.tensor_tensor(both[:], forward[1, 1][:], backward[1, 1][:], ALU.add)
+        backward[1, 1] = both
+        summed = fused + [(1, 1)]
+        for b in range(2, BLOCKS):
             for h in range(HALVES):
-                backward[b, h] = keep.tile([P, HALF], F32, name=f"backward{b}_{h}")
-                nc.scalar.activation(backward[b, h][:], looked_up(betas[b], en_list, h * HALF, HALF), COPY)
+                gather_backward(b, h)
 
-        def largest_of_groups(b):
-            pairs = keep.tile([P, W, 2], F32, name=f"pairs{b}")
-            quads = metric[b][:].rearrange("p (g u e) -> p g u e", u=2, e=2)
-            nc.vector.tensor_tensor(pairs[:], quads[:, :, 0, :], quads[:, :, 1, :], ALU.max)
-            nc.vector.tensor_tensor(best[b][:, :W], pairs[:, :, 0], pairs[:, :, 1], ALU.max)
-
-        metric, started = {}, {}
         for b in range(BLOCKS):
             c, cols = b // 2, slice((b % 2) * P, (b % 2 + 1) * P)
-            metric[b] = keep.tile([P, S], F32, name=f"metric{b}")
+            metric, pairs = {}, {}
             for h in range(HALVES):
                 y = psum.tile([P, HALF], F32, name=f"y{b}_{h}")
                 nc.tensor.matmul_mx(
@@ -143,24 +155,28 @@ def tile_picked_ybcjr_max_p_kernel(tc, x_words, x_scales, hT, alpha, beta, prior
                     start=True,
                     stop=True,
                 )
-                if b == 0:
-                    nc.vector.tensor_tensor(metric[b][:, h * HALF : (h + 1) * HALF], y[:], backward[b, h][:], ALU.add)
-                else:
-                    started[b, h] = keep.tile([P, HALF], F32, name=f"started{b}_{h}")
-                    nc.vector.tensor_tensor(started[b, h][:], y[:], forward[b, h][:], ALU.add)
-            if b == 0:
-                largest_of_groups(b)
-        for b in range(1, BLOCKS):
+                metric[h] = keep.tile([P, HALF], F32, name=f"metric{b}_{h}")
+                first = backward[b, h] if (b, h) in summed else forward[b, h]
+                nc.vector.tensor_tensor(metric[h][:], y[:], first[:], ALU.add)
             for h in range(HALVES):
-                nc.vector.tensor_tensor(metric[b][:, h * HALF : (h + 1) * HALF], started[b, h][:], backward[b, h][:], ALU.add)
-            largest_of_groups(b)
+                if (b, h) not in summed:
+                    whole = keep.tile([P, HALF], F32, name=f"whole{b}_{h}")
+                    nc.vector.tensor_tensor(whole[:], metric[h][:], backward[b, h][:], ALU.add)
+                    metric[h] = whole
+            for h in range(HALVES):
+                pairs[h] = keep.tile([P, HALF // D, 2], F32, name=f"pairs{b}_{h}")
+                quads = metric[h][:].rearrange("p (g u e) -> p g u e", u=2, e=2)
+                nc.vector.tensor_tensor(pairs[h][:], quads[:, :, 0, :], quads[:, :, 1, :], ALU.max)
+            for h in range(HALVES):
+                groups = slice(h * (HALF // D), (h + 1) * (HALF // D))
+                nc.vector.tensor_tensor(best[b][:, groups], pairs[h][:, :, 0], pairs[h][:, :, 1], ALU.max)
 
         for b in range(BLOCKS):
             ones = keep.tile([P, W], F32, name=f"ones{b}")
             part = keep.tile([P, W], F32, name=f"part{b}")
             result = keep.tile([P, W], F32, name=f"result{b}")
             nc.scalar.activation(ones[:], looked_up(best[b], one_list, 0, W), COPY, scale=GAIN)
-            if b < 3:
+            if b < 4:
                 zeros = keep.tile([P, W], F32, name=f"zeros{b}")
                 nc.scalar.activation(zeros[:], looked_up(best[b], zero_list, 0, W), COPY, scale=GAIN)
                 nc.vector.scalar_tensor_tensor(part[:], priors[:, b, :], -GAIN, ones[:], ALU.mult, ALU.add)

@@ -52,9 +52,6 @@ def tile_picked_ybcjr_max_p_kernel(tc, x_words, x_scales, hT, alpha, beta, prior
             nc.sync.dma_start(tile[:], hT[:, c * (V // 2) : (c + 1) * (V // 2)].rearrange("(p j) t -> p j t", j=PACK))
             return tile
 
-        warm = keep.tile([P, 8], F32, name="warm")
-        nc.gpsimd.memset(warm[:, 0:1], 0.0)
-        nc.scalar.activation(warm[:, 4:5], warm[:, 0:1], COPY)
 
         alphas, betas, h_raw = {}, {}, {}
         st_list = load_list("st_list", st)

from contextlib import ExitStack

import concourse.mybir as mybir

K, T, S, V, D, R, W = 512, 4096, 1024, 512, 4, 256, 256
FLOPS = 2 * K * V * S

F32 = mybir.dt.float32
BF16 = mybir.dt.bfloat16
I32 = mybir.dt.int32
U32 = mybir.dt.uint32
U16 = mybir.dt.uint16
U8 = mybir.dt.uint8
FP8X4 = mybir.dt.float8_e4m3fn_x4
ALU = mybir.AluOpType
COPY = mybir.ActivationFunctionType.Copy

P = 128
PACK = 4
BLOCKS = V // P
HALF = 512
HALVES = S // HALF
STRIPE = 16
GAIN = 0.7
STATE_WINDOW = HALF + STRIPE
BIT_WINDOW = W + STRIPE


def looked_up(window, offsets, first, count):
    return window[:].indirect(offsets[:, first // STRIPE : (first + count) // STRIPE])


def tile_picked_ybcjr_max_p_kernel(tc, x_words, x_scales, hT, alpha, beta, prior, offs, st, en, one, zero, out):
    nc = tc.nc
    with ExitStack() as ctx:
        keep = ctx.enter_context(tc.tile_pool(name="keep", bufs=1))
        psum = ctx.enter_context(tc.psum_pool(name="psum", bufs=1))

        def load_list(name, source):
            tile = keep.tile(list(source.shape), U16, name=name)
            nc.sync.dma_start(tile[:], source)
            return tile

        def load_states(name, source, b):
            tile = keep.tile([P, STATE_WINDOW], F32, name=f"{name}{b}")
            (nc.vector if b == 0 else nc.gpsimd).memset(tile[:, R:], 0.0)
            nc.sync.dma_start(tile[:, :R], source[b * P : (b + 1) * P, :])
            return tile

        def load_h(c):
            tile = keep.tile([P, PACK, V // 2], F32, name=f"h_raw{c}")
            nc.sync.dma_start(tile[:], hT[:, c * (V // 2) : (c + 1) * (V // 2)].rearrange("(p j) t -> p j t", j=PACK))
            return tile


        alphas, betas, h_raw = {}, {}, {}
        st_list = load_list("st_list", st)
        alphas[0] = load_states("alpha", alpha, 0)
        en_list = load_list("en_list", en)
        betas[0] = load_states("beta", beta, 0)
        alphas[1] = load_states("alpha", alpha, 1)
        betas[1] = load_states("beta", beta, 1)
        offs_list = load_list("offs_list", offs)
        word_table = keep.tile([P, T], U32, name="word_table")
        nc.sync.dma_start(word_table[:].bitcast(I32), x_words[0].rearrange("p c r -> p (c r)").bitcast(I32))
        alphas[2] = load_states("alpha", alpha, 2)
        scale_table = keep.tile([P, T], U8, name="scale_table")
        nc.vector.memset(scale_table[:].bitcast(I32), 0)
        for q in range(4):
            nc.sync.dma_start(scale_table[32 * q : 32 * q + 4, :].bitcast(I32), x_scales[0, 4 * q : 4 * q + 4, :].bitcast(I32))
        h_raw[0] = load_h(0)
        alphas[3] = load_states("alpha", alpha, 3)
        h_raw[1] = load_h(1)
        for b in range(2, BLOCKS):
            betas[b] = load_states("beta", beta, b)
        priors = keep.tile([P, BLOCKS, W], F32, name="priors")
        nc.sync.dma_start(priors[:], prior.rearrange("(b p) g -> p b g", p=P))
        one_list = load_list("one_list", one)
        zero_list = load_list("zero_list", zero)

        best = {}
        for b in range(BLOCKS):
            best[b] = keep.tile([P, BIT_WINDOW], F32, name=f"best{b}")
            nc.gpsimd.memset(best[b][:, W:], 0.0)

        x_codes, x_bytes = {}, {}
        forward, backward = {}, {}
        fused = [(0, 0), (0, 1), (1, 0)]

        def gather_forward(b, h):
            forward[b, h] = keep.tile([P, HALF], F32, name=f"forward{b}_{h}")
            if (b, h) == (0, 1):
                nc.vector.tensor_copy(forward[b, h][:], looked_up(alphas[b], st_list, h * HALF, HALF))
            else:
                nc.scalar.activation(forward[b, h][:], looked_up(alphas[b], st_list, h * HALF, HALF), COPY)

        def gather_backward(b, h):
            backward[b, h] = keep.tile([P, HALF], F32, name=f"backward{b}_{h}")
            if (b, h) in fused:
                nc.vector.tensor_tensor(backward[b, h][:], looked_up(betas[b], en_list, h * HALF, HALF), forward[b, h][:], ALU.add)
            else:
                nc.scalar.activation(backward[b, h][:], looked_up(betas[b], en_list, h * HALF, HALF), COPY)

        for b in range(2):
            for h in range(HALVES):
                gather_forward(b, h)
        for b in range(2):
            for h in range(HALVES):
                gather_backward(b, h)
        for b in range(2, BLOCKS):
            for h in range(HALVES):
                gather_forward(b, h)

        for h in range(HALVES):
            x_codes[h] = keep.tile([P, HALF], U32, name=f"x_codes{h}", align_bytes=64)
            nc.vector.tensor_copy(x_codes[h][:], looked_up(word_table, offs_list, h * HALF, HALF))

        for h in range(HALVES):
            x_bytes[h] = keep.tile([P, HALF], U8, name=f"x_bytes{h}", align_bytes=64)
            nc.vector.tensor_copy(x_bytes[h][:], looked_up(scale_table, offs_list, h * HALF, HALF))

        h_codes, h_bytes = {}, {}
        for c in range(2):
            rounded = keep.tile([P, V // 2, PACK], BF16, name=f"h_rounded{c}", tag=f"h_rounded{c}", align_bytes=64)
            (nc.scalar.copy if c in [0,1] else nc.vector.tensor_copy)(
                rounded[:].rearrange("p (c i) j -> p c j i", i=4),
                h_raw[c][:].rearrange("p j (c i) -> p c j i", i=4),
            )
            h_codes[c] = keep.tile([P, V // 2], U32, name=f"h_codes{c}", align_bytes=64)
            h_bytes[c] = keep.tile([P, V // 2], U8, name=f"h_bytes{c}", align_bytes=64)
            nc.vector.quantize_mx(out=h_codes[c][:].bitcast(FP8X4), scales=h_bytes[c][:], in_=rounded[:].rearrange("p t j -> p (t j)"))

        both = keep.tile([P, HALF], F32, name="both", tag="h_rounded0", align_bytes=64)
        nc.vector.tensor_tensor(both[:], forward[1, 1][:], backward[1, 1][:], ALU.add)
        backward[1, 1] = both
        summed = fused + [(1, 1)]
        for b in range(2, BLOCKS):
            for h in range(HALVES):
                gather_backward(b, h)

        for b in range(BLOCKS):
            c, cols = b // 2, slice((b % 2) * P, (b % 2 + 1) * P)
            metric, pairs = {}, {}
            for h in range(HALVES):
                y = psum.tile([P, HALF], F32, name=f"y{b}_{h}")
                nc.tensor.matmul_mx(
                    out=y[:],
                    lhsT=h_codes[c][:, cols].bitcast(FP8X4),
                    lhsT_scale=h_bytes[c][:, cols],
                    rhs=x_codes[h][:].bitcast(FP8X4),
                    rhs_scale=x_bytes[h][:],
                    start=True,
                    stop=True,
                )
                metric[h] = keep.tile([P, HALF], F32, name=f"metric{b}_{h}")
                first = backward[b, h] if (b, h) in summed else forward[b, h]
                nc.vector.tensor_tensor(metric[h][:], y[:], first[:], ALU.add)
            for h in range(HALVES):
                if (b, h) not in summed:
                    whole = keep.tile([P, HALF], F32, name=f"whole{b}_{h}")
                    nc.vector.tensor_tensor(whole[:], metric[h][:], backward[b, h][:], ALU.add)
                    metric[h] = whole
            for h in range(HALVES):
                pairs[h] = keep.tile([P, HALF // D, 2], F32, name=f"pairs{b}_{h}")
                quads = metric[h][:].rearrange("p (g u e) -> p g u e", u=2, e=2)
                nc.vector.tensor_tensor(pairs[h][:], quads[:, :, 0, :], quads[:, :, 1, :], ALU.max)
            for h in range(HALVES):
                groups = slice(h * (HALF // D), (h + 1) * (HALF // D))
                nc.vector.tensor_tensor(best[b][:, groups], pairs[h][:, :, 0], pairs[h][:, :, 1], ALU.max)

        for b in range(BLOCKS):
            ones = keep.tile([P, W], F32, name=f"ones{b}")
            part = keep.tile([P, W], F32, name=f"part{b}")
            result = keep.tile([P, W], F32, name=f"result{b}")
            nc.scalar.activation(ones[:], looked_up(best[b], one_list, 0, W), COPY, scale=GAIN)
            if b < 4:
                zeros = keep.tile([P, W], F32, name=f"zeros{b}")
                nc.scalar.activation(zeros[:], looked_up(best[b], zero_list, 0, W), COPY, scale=GAIN)
                nc.vector.scalar_tensor_tensor(part[:], priors[:, b, :], -GAIN, ones[:], ALU.mult, ALU.add)
                nc.vector.tensor_tensor(result[:], part[:], zeros[:], ALU.subtract)
            else:
                nc.vector.tensor_tensor(part[:], looked_up(best[b], zero_list, 0, W), priors[:, b, :], ALU.add)
                nc.vector.scalar_tensor_tensor(result[:], part[:], -GAIN, ones[:], ALU.mult, ALU.add)
            nc.sync.dma_start(out[b * P : (b + 1) * P, :], result[:])
